import numpy as np
import ml_dtypes


def mxq(x, axis, fmt="e4m3"):
    dtype, down = {"e4m3": (ml_dtypes.float8_e4m3fn, 7), "e5m2": (ml_dtypes.float8_e5m2, 14)}[fmt]
    v = np.moveaxis(np.asarray(x, np.float32).astype(ml_dtypes.bfloat16).astype(np.float64), axis, -1)
    blocks = v.reshape(v.shape[:-1] + (-1, 32))
    amax = np.abs(blocks).max(-1, keepdims=True)
    byte = np.maximum(np.where(amax > 0, np.frexp(amax)[1] - 1 + 127, 0) - down, 1)
    scale = np.exp2(byte - 127.0)
    codes = (blocks / scale).astype(np.float32).astype(dtype).astype(np.float64)
    return np.moveaxis((codes * scale).reshape(v.shape), -1, axis)


WIDE = False


def mx_kscale(k):
    if not WIDE:
        return np.ones(k)
    levels = np.array([10, -10, 5, -5, 0])
    if k % 512:
        return np.exp2(np.random.permutation(np.resize(levels, k // 32))).repeat(32)
    a = np.empty((k // 512, 16))
    for p in range(k // 512):
        a[p, :8] = np.random.permutation(np.resize(levels, 8))
        for g in range(8):
            far = levels[np.abs(levels - a[p, g]) >= 10]
            a[p, g + 8] = far[np.random.randint(len(far))]
    return np.exp2(a.ravel()).repeat(32)


def f64(x):
    return np.asarray(x).astype(np.float64)


def striped(idx):
    return np.tile(idx.reshape(-1, 16).T, (8, 1)).astype(np.uint16)


def unstriped(offs):
    return offs[:16].T.reshape(-1).astype(np.int64)


E2M1 = np.array([0.0, 0.5, 1.0, 1.5, 2.0, 3.0, 4.0, 6.0, -0.0, -0.5, -1.0, -1.5, -2.0, -3.0, -4.0, -6.0])


def pack_weight(w, fmt):
    k, n = w.shape
    w = f64(np.asarray(w, np.float32).astype(ml_dtypes.bfloat16)).reshape(k // 32, 32, n)
    amax = np.abs(w).max(1)
    if fmt == "e4m3":
        byte = np.frexp(amax)[1] - 1 + 127 - 7
    else:
        mant, ex = np.frexp(amax / 6.0)
        byte = np.where(mant > 0.5, ex, ex - 1) + 127
    byte = np.clip(np.where(amax > 0, byte, 1), 1, 254)
    scaled = (w * np.exp2(127.0 - byte)[:, None, :]).reshape(k, n).astype(np.float32)
    by_word = np.ascontiguousarray(scaled.reshape(k // 512, 128, 4, n).transpose(0, 1, 3, 2))
    if fmt == "e4m3":
        words = by_word.astype(ml_dtypes.float8_e4m3fn).view(np.uint8)
    else:
        c = by_word.astype(ml_dtypes.float4_e2m1fn).view(np.uint8) & 0xF
        words = (c[..., 0::2] | (c[..., 1::2] << 4)).reshape(k // 512, 128, 2 * n)
    return np.ascontiguousarray(words), np.ascontiguousarray(byte.astype(np.uint8).reshape(k // 512, 16, n))


def unpack_weight(words, scales, fmt):
    g, _, n = scales.shape
    words = np.ascontiguousarray(words).reshape(g, 128, n, -1)
    if fmt == "e4m3":
        vals = words.view(ml_dtypes.float8_e4m3fn).astype(np.float64)
    else:
        nib = np.empty((g, 128, n, 4), np.uint8)
        nib[..., 0::2] = words & 0xF
        nib[..., 1::2] = words >> 4
        vals = E2M1[nib]
    vals = vals * np.repeat(np.exp2(scales.astype(np.float64) - 127.0), 8, axis=1)[..., None]
    return vals.transpose(0, 1, 3, 2).reshape(g * 512, n)


def gelu(v):
    return 0.5 * v * (1.0 + np.tanh(np.sqrt(2.0 / np.pi) * (v + 0.044715 * v**3)))


K, H, T, S, T3, S2, P = 1536, 1024, 4096, 1024, 2048, 512, 512

def setup_inputs():
    n = np.random.standard_normal
    s = mx_kscale(K)[:, None]
    u = mx_kscale(H)[:, None]
    d = {}
    d["tab_words"], d["tab_scales"] = pack_weight(n((K, T)) * s, "e4m3")
    d["offs"] = striped(np.random.permutation(T)[:S])
    d["tab2_words"], d["tab2_scales"] = pack_weight(1.3 * n((H, T3)) / H**0.5 / u, "e4m3")
    d["offs2"] = striped(np.random.permutation(T3)[:S2])
    d["pos1"] = striped(np.random.permutation(S)[:P])
    d["pos2"] = striped(np.random.permutation(S)[:P])
    d["w1"] = (1.5 * n((K, H)) / K**0.5 / s).astype(np.float32)
    d["gain"] = (np.exp(0.4 * n(H)) * u[:, 0]).astype(np.float32)
    d["w4_words"], d["w4_scales"] = pack_weight(1.5 * n((H, S2)) / H**0.5 / u, "e2m1")
    d["setting"] = (0.8 * n(S2)).astype(np.float32)
    return d

def reference(tab_words, tab_scales, offs, tab2_words, tab2_scales, offs2, pos1, pos2, w1, gain, w4_words, w4_scales, setting):
    v = unpack_weight(tab_words, tab_scales, "e4m3")[:, unstriped(offs)]
    v2 = unpack_weight(tab2_words, tab2_scales, "e4m3")[:, unstriped(offs2)]
    w4 = unpack_weight(w4_words, w4_scales, "e2m1")
    h = np.tanh(mxq(f64(w1), 0, "e4m3").T @ v) * f64(gain)[:, None]
    hq = mxq(h, 0, "e4m3")
    e = v2.T @ hq
    f = w4.T @ hq
    score = e * f
    bare = np.abs(score[:, unstriped(pos1)])
    fletched = np.abs(score[:, unstriped(pos2)])
    return bare - fletched + f64(setting)[:, None]

@@ -1,0 +1,264 @@
+from contextlib import ExitStack
+
+import concourse.mybir as mybir
+
+K, H, T, S, T3, S2, NP = 1536, 1024, 4096, 1024, 2048, 512, 512
+FLOPS = 2 * K * H * S + 2 * 2 * H * S2 * S
+
+F32 = mybir.dt.float32
+BF16 = mybir.dt.bfloat16
+I32 = mybir.dt.int32
+U32 = mybir.dt.uint32
+U16 = mybir.dt.uint16
+U8 = mybir.dt.uint8
+FP8X4 = mybir.dt.float8_e4m3fn_x4
+FP4X4 = mybir.dt.float4_e2m1fn_x4
+ACT = mybir.ActivationFunctionType
+ALU = mybir.AluOpType
+
+P = 128
+PACK = 4
+PASS = P * PACK
+KP = K // PASS
+HP = H // PASS
+BANKS = 8
+JB = S // BANKS
+HALF = 512
+MT = S2 // P
+
+
+def tile_list_bare_fletched_contrast_kernel(
+    tc, tab_words, tab_scales, offs, tab2_words, tab2_scales, offs2, pos1, pos2,
+    w1, gain, w4_words, w4_scales, setting, out,
+):
+    nc = tc.nc
+    with ExitStack() as ctx:
+        keep = ctx.enter_context(tc.tile_pool(name="keep", bufs=1))
+        ring = ctx.enter_context(tc.tile_pool(name="ring", bufs=2))
+        psum = ctx.enter_context(tc.psum_pool(name="psum", bufs=1))
+
+        def kept(shape, dtype, name):
+            return keep.tile(shape, dtype, name=name, align_bytes=64)
+
+        offs_sb = keep.tile([P, S // 16], U16, name="offs_sb")
+        offs2_sb = keep.tile([P, S2 // 16], U16, name="offs2_sb")
+        pos1_sb = keep.tile([P, NP // 16], U16, name="pos1_sb")
+        pos2_sb = keep.tile([P, NP // 16], U16, name="pos2_sb")
+        tab_w = [kept([P, T], U32, "tab_w%d" % a) for a in range(KP)]
+        tab_s = kept([P, T], U8, "tab_s")
+        tab2_w = [kept([P, T3], U32, "tab2_w%d" % b) for b in range(HP)]
+        tab2_s = kept([P, T3], U8, "tab2_s")
+        w4_w = kept([P, HP, 2 * S2], U8, "w4_w")
+        w4_s = kept([P, HP, S2], U8, "w4_s")
+        w_raw = {(b, a): kept([P, PACK, PASS], F32, "w_raw%d%d" % (b, a)) for b in range(HP) for a in range(KP)}
+        gain_sb = kept([P, HP, PACK], F32, "gain_sb")
+        set_sb = kept([P, MT], F32, "set_sb")
+
+        nc.vector.memset(tab_s[:].bitcast(I32), 0)
+        nc.vector.memset(tab2_s[:].bitcast(I32), 0)
+        nc.vector.memset(w4_s[:].rearrange("p a n -> p (a n)").bitcast(I32), 0)
+        def load_words(dst, src):
+            nc.sync.dma_start(out=dst[:].bitcast(I32), in_=src.rearrange("p n t -> p (n t)").bitcast(I32))
+
+        def load_w1(b, a):
+            rows = w1[a * PASS : (a + 1) * PASS, b * PASS : (b + 1) * PASS]
+            nc.sync.dma_start(out=w_raw[b, a][:], in_=rows.rearrange("(p i) c -> p i c", i=PACK))
+
+        nc.sync.dma_start(offs_sb[:], offs)
+        nc.sync.dma_start(offs2_sb[:], offs2)
+        nc.sync.dma_start(pos2_sb[:], pos2)
+        nc.sync.dma_start(pos1_sb[:], pos1)
+        load_words(tab_w[0], tab_words[0])
+        for q in range(4):
+            nc.sync.dma_start(out=tab_s[32 * q : 32 * q + 4 * KP, :].bitcast(I32),
+                              in_=tab_scales[:, 4 * q : 4 * q + 4, :].bitcast(I32))
+        load_w1(0, 0)
+        load_w1(0, 1)
+        nc.sync.dma_start(out=gain_sb[:], in_=gain.rearrange("(b p t) -> p b t", p=P, t=PACK))
+        load_words(tab_w[1], tab_words[1])
+        load_w1(0, 2)
+        load_words(tab_w[2], tab_words[2])
+        load_w1(1, 0)
+        load_w1(1, 1)
+        load_w1(1, 2)
+        for q in range(4):
+            nc.sync.dma_start(out=tab2_s[32 * q : 32 * q + 4 * HP, :].bitcast(I32),
+                              in_=tab2_scales[:, 4 * q : 4 * q + 4, :].bitcast(I32))
+        load_words(tab2_w[0], tab2_words[0])
+        load_words(tab2_w[1], tab2_words[1])
+        nc.sync.dma_start(out=w4_w[:].bitcast(I32), in_=w4_words.rearrange("a p n -> p a n").bitcast(I32))
+        for q in range(4):
+            nc.sync.dma_start(out=w4_s[32 * q : 32 * q + 4, :, :].bitcast(I32),
+                              in_=w4_scales[:, 4 * q : 4 * q + 4, :].rearrange("a r n -> r a n").bitcast(I32))
+        with nc.allow_non_contiguous_dma(reason="one offset a partition"):
+            nc.sync.dma_start(out=set_sb[:], in_=setting.rearrange("(m p) -> p m", p=P))
+
+        v_w = [[kept([P, HALF], U32, "v_w%d%d" % (a, h)) for h in range(2)] for a in range(KP)]
+        v_s = kept([P, S], U8, "v_s")
+        v2_w = [kept([P, S2], U32, "v2_w%d" % b) for b in range(HP)]
+        v2_s = kept([P, S2], U8, "v2_s")
+        wq_w = {key: kept([P, PASS], U32, "wq_w%d%d" % key) for key in w_raw}
+        wq_s = {key: kept([P, PASS], U8, "wq_s%d%d" % key) for key in w_raw}
+        hq_w = {(b, h): kept([P, HALF], U32, "hq_w%d%d" % (b, h)) for b in range(HP) for h in range(2)}
+        hq_s = {(b, h): kept([P, HALF], U8, "hq_s%d%d" % (b, h)) for b in range(HP) for h in range(2)}
+
+        def gather_v(a, h):
+            cols = HALF // 16
+            nc.vector.tensor_copy(v_w[a][h][:], tab_w[a][:].indirect(offs_sb[:, h * cols : (h + 1) * cols]))
+
+        w_bf = {}
+
+        def cast_w1(b, a, on_vector):
+            w_bf[b, a] = ring.tile([P, PACK, P, PACK], BF16, name="w_bf", align_bytes=64)
+            src = w_raw[b, a][:].rearrange("p i (m t) -> p m i t", t=PACK)
+            dst = w_bf[b, a][:].rearrange("p t m i -> p m i t")
+            if on_vector:
+                nc.vector.tensor_copy(out=dst, in_=src)
+            else:
+                nc.scalar.copy(out=dst, in_=src)
+
+        def quant_w1(b, a):
+            nc.vector.quantize_mx(out=wq_w[b, a][:].bitcast(FP8X4), scales=wq_s[b, a][:],
+                                  in_=w_bf[b, a][:].rearrange("p t m i -> p (t m i)"))
+
+        pre = {}
+
+        def stage1(b, a, jb):
+            if a == 0:
+                pre[b, jb] = psum.tile([P, PACK, JB], F32, name="bank%d" % jb)
+            h, j0 = divmod(jb * JB, HALF)
+            for t in range(PACK):
+                nc.tensor.matmul_mx(
+                    out=pre[b, jb][:, t, :],
+                    lhsT=wq_w[b, a][:, t * P : (t + 1) * P].bitcast(FP8X4),
+                    lhsT_scale=wq_s[b, a][:, t * P : (t + 1) * P],
+                    rhs=v_w[a][h][:, j0 : j0 + JB].bitcast(FP8X4),
+                    rhs_scale=v_s[4 * a :, jb * JB : (jb + 1) * JB],
+                    start=(a == 0 and t == 0),
+                    stop=(a == KP - 1 and t == PACK - 1),
+                )
+
+        h_bf = {}
+
+        def features(b, jb):
+            h, j0 = divmod(jb * JB, HALF)
+            if j0 == 0:
+                h_bf[b, h] = ring.tile([P, HALF, PACK], BF16, name="h_bf", align_bytes=64)
+            th = ring.tile([P, JB, PACK], F32, name="th", bufs=6)
+            nc.scalar.activation(out=th[:], in_=pre[b, jb][:].rearrange("p t j -> p j t"), func=ACT.Tanh)
+            nc.vector.tensor_tensor(out=h_bf[b, h][:, j0 : j0 + JB, :], in0=th[:],
+                                    in1=gain_sb[:, b : b + 1, :].to_broadcast([P, JB, PACK]), op=ALU.mult)
+
+        def quant_h(b, jb):
+            h, j0 = divmod(jb * JB, HALF)
+            nc.vector.quantize_mx(out=hq_w[b, h][:, j0 : j0 + JB].bitcast(FP8X4), scales=hq_s[b, h][:, j0 : j0 + JB],
+                                  in_=h_bf[b, h][:, j0 : j0 + JB, :].rearrange("p j t -> p (j t)"))
+
+        def feature_step(b, jb):
+            features(b, jb)
+            if jb > 0:
+                quant_h(b, jb - 1)
+
+        gather_v(0, 0)
+        gather_v(0, 1)
+        cast_w1(0, 0, False)
+        quant_w1(0, 0)
+        nc.vector.tensor_copy(v_s[:], tab_s[:].indirect(offs_sb[:]))
+        cast_w1(0, 1, False)
+        quant_w1(0, 1)
+        gather_v(1, 0)
+        gather_v(1, 1)
+        cast_w1(0, 2, False)
+        quant_w1(0, 2)
+        gather_v(2, 0)
+        gather_v(2, 1)
+        for a in range(KP):
+            for jb in range(BANKS):
+                stage1(0, a, jb)
+        cast_w1(1, 0, True)
+        feature_step(0, 0)
+        quant_w1(1, 0)
+        for jb in range(1, 4):
+            feature_step(0, jb)
+        cast_w1(1, 1, False)
+        feature_step(0, 4)
+        quant_w1(1, 1)
+        for jb in range(5, BANKS):
+            feature_step(0, jb)
+        cast_w1(1, 2, False)
+        nc.vector.tensor_copy(v2_s[:], tab2_s[:].indirect(offs2_sb[:]))
+        quant_h(0, BANKS - 1)
+        quant_w1(1, 2)
+        nc.vector.tensor_copy(v2_w[0][:], tab2_w[0][:].indirect(offs2_sb[:]))
+        nc.vector.tensor_copy(v2_w[1][:], tab2_w[1][:].indirect(offs2_sb[:]))
+        for jb in range(BANKS):
+            for a in range(KP):
+                stage1(1, a, jb)
+        for jb in range(BANKS):
+            feature_step(1, jb)
+        quant_h(1, BANKS - 1)
+
+        size = {}
+        rest = {}
+        order = [(0, 0), (1, 0), (0, 1), (1, 1), (2, 0), (2, 1), (3, 0), (3, 1)]
+
+        def scores(m, h):
+            first = 2 * order.index((m, h)) % BANKS
+            abs_e = ring.tile([P, HALF], F32, name="abs_e", bufs=4)
+            abs_f = ring.tile([P, HALF], F32, name="abs_f", bufs=4)
+            f_ps = psum.tile([P, HALF], F32, name="bank%d" % first)
+            e_ps = psum.tile([P, HALF], F32, name="bank%d" % (first + 1))
+            for b in range(HP):
+                nc.tensor.matmul_mx(
+                    out=f_ps[:], lhsT=w4_w[:, b, 2 * m * P : 2 * (m + 1) * P].bitcast(FP4X4),
+                    lhsT_scale=w4_s[:, b, m * P : (m + 1) * P],
+                    rhs=hq_w[b, h][:].bitcast(FP8X4), rhs_scale=hq_s[b, h][:],
+                    start=(b == 0), stop=(b == HP - 1))
+            for b in range(HP):
+                nc.tensor.matmul_mx(
+                    out=e_ps[:], lhsT=v2_w[b][:, m * P : (m + 1) * P].bitcast(FP8X4),
+                    lhsT_scale=v2_s[4 * b :, m * P : (m + 1) * P],
+                    rhs=hq_w[b, h][:].bitcast(FP8X4), rhs_scale=hq_s[b, h][:],
+                    start=(b == 0), stop=(b == HP - 1))
+            nc.scalar.activation(out=abs_f[:], in_=f_ps[:], func=ACT.Abs)
+            nc.scalar.activation(out=abs_e[:], in_=e_ps[:], func=ACT.Abs)
+            if h == 0:
+                size[m] = ring.tile([P, S], F32, name="size", bufs=3)
+            nc.vector.tensor_tensor(out=size[m][:, h * HALF : (h + 1) * HALF], in0=abs_e[:], in1=abs_f[:], op=ALU.mult)
+
+        fletched = {}
+
+        def pick_fletched(m):
+            fletched[m] = ring.tile([P, NP], F32, name="fletched")
+            nc.vector.tensor_copy(fletched[m][:], size[m][:].indirect(pos2_sb[:]))
+
+        def offset_fletched(m):
+            rest[m] = ring.tile([P, NP], F32, name="rest")
+            nc.scalar.activation(out=rest[m][:], in_=fletched[m][:], func=ACT.Identity,
+                                 bias=set_sb[:, m : m + 1], scale=-1.0)
+
+        def pick_bare(m):
+            res = ring.tile([P, NP], F32, name="res")
+            nc.vector.tensor_tensor(out=res[:], in0=size[m][:].indirect(pos1_sb[:]), in1=rest[m][:], op=ALU.add)
+            nc.sync.dma_start(out=out[m * P : (m + 1) * P, :], in_=res[:])
+
+        scores(0, 0)
+        scores(1, 0)
+        scores(0, 1)
+        pick_fletched(0)
+        scores(1, 1)
+        offset_fletched(0)
+        pick_fletched(1)
+        pick_bare(0)
+        scores(2, 0)
+        scores(2, 1)
+        offset_fletched(1)
+        pick_fletched(2)
+        pick_bare(1)
+        scores(3, 0)
+        scores(3, 1)
+        offset_fletched(2)
+        pick_fletched(3)
+        offset_fletched(3)
+        pick_bare(2)
+        pick_bare(3)

@@ -64,15 +64,19 @@ def tile_list_bare_fletched_contrast_kernel(
             rows = w1[a * PASS : (a + 1) * PASS, b * PASS : (b + 1) * PASS]
             nc.sync.dma_start(out=w_raw[b, a][:], in_=rows.rearrange("(p i) c -> p i c", i=PACK))
 
-        nc.sync.dma_start(offs_sb[:], offs)
-        nc.sync.dma_start(offs2_sb[:], offs2)
-        nc.sync.dma_start(pos2_sb[:], pos2)
-        nc.sync.dma_start(pos1_sb[:], pos1)
-        load_words(tab_w[0], tab_words[0])
         for q in range(4):
-            nc.sync.dma_start(out=tab_s[32 * q : 32 * q + 4 * KP, :].bitcast(I32),
-                              in_=tab_scales[:, 4 * q : 4 * q + 4, :].bitcast(I32))
+            nc.gpsimd.dma_start(out=tab_s[32 * q : 32 * q + 4 * KP, :].bitcast(I32),
+                                in_=tab_scales[:, 4 * q : 4 * q + 4, :].bitcast(I32))
+        for q in range(4):
+            nc.gpsimd.dma_start(out=tab2_s[32 * q : 32 * q + 4 * HP, :].bitcast(I32),
+                                in_=tab2_scales[:, 4 * q : 4 * q + 4, :].bitcast(I32))
+        for q in range(4):
+            nc.gpsimd.dma_start(out=w4_s[32 * q : 32 * q + 4, :, :].bitcast(I32),
+                                in_=w4_scales[:, 4 * q : 4 * q + 4, :].rearrange("a r n -> r a n").bitcast(I32))
+        load_words(tab_w[0], tab_words[0])
+        nc.sync.dma_start(offs_sb[:], offs)
         load_w1(0, 0)
+        nc.sync.dma_start(offs2_sb[:], offs2)
         load_w1(0, 1)
         nc.sync.dma_start(out=gain_sb[:], in_=gain.rearrange("(b p t) -> p b t", p=P, t=PACK))
         load_words(tab_w[1], tab_words[1])
@@ -81,15 +85,11 @@ def tile_list_bare_fletched_contrast_kernel(
         load_w1(1, 0)
         load_w1(1, 1)
         load_w1(1, 2)
-        for q in range(4):
-            nc.sync.dma_start(out=tab2_s[32 * q : 32 * q + 4 * HP, :].bitcast(I32),
-                              in_=tab2_scales[:, 4 * q : 4 * q + 4, :].bitcast(I32))
         load_words(tab2_w[0], tab2_words[0])
         load_words(tab2_w[1], tab2_words[1])
         nc.sync.dma_start(out=w4_w[:].bitcast(I32), in_=w4_words.rearrange("a p n -> p a n").bitcast(I32))
-        for q in range(4):
-            nc.sync.dma_start(out=w4_s[32 * q : 32 * q + 4, :, :].bitcast(I32),
-                              in_=w4_scales[:, 4 * q : 4 * q + 4, :].rearrange("a r n -> r a n").bitcast(I32))
+        nc.sync.dma_start(pos2_sb[:], pos2)
+        nc.sync.dma_start(pos1_sb[:], pos1)
         with nc.allow_non_contiguous_dma(reason="one offset a partition"):
             nc.sync.dma_start(out=set_sb[:], in_=setting.rearrange("(m p) -> p m", p=P))
 
@@ -110,8 +110,8 @@ def tile_list_bare_fletched_contrast_kernel(
 
         def cast_w1(b, a, on_vector):
             w_bf[b, a] = ring.tile([P, PACK, P, PACK], BF16, name="w_bf", align_bytes=64)
-            src = w_raw[b, a][:].rearrange("p i (m t) -> p m i t", t=PACK)
-            dst = w_bf[b, a][:].rearrange("p t m i -> p m i t")
+            src = w_raw[b, a][:].rearrange("p i (m u v) -> p u m i v", u=2, v=2)
+            dst = w_bf[b, a][:].rearrange("p (u v) m i -> p u m i v", v=2)
             if on_vector:
                 nc.vector.tensor_copy(out=dst, in_=src)
             else:

@@ -85,9 +85,9 @@ def tile_list_bare_fletched_contrast_kernel(
         load_w1(1, 0)
         load_w1(1, 1)
         load_w1(1, 2)
+        nc.sync.dma_start(out=w4_w[:].bitcast(I32), in_=w4_words.rearrange("a p n -> p a n").bitcast(I32))
         load_words(tab2_w[0], tab2_words[0])
         load_words(tab2_w[1], tab2_words[1])
-        nc.sync.dma_start(out=w4_w[:].bitcast(I32), in_=w4_words.rearrange("a p n -> p a n").bitcast(I32))
         nc.sync.dma_start(pos2_sb[:], pos2)
         nc.sync.dma_start(pos1_sb[:], pos1)
         with nc.allow_non_contiguous_dma(reason="one offset a partition"):
@@ -199,66 +199,59 @@ def tile_list_bare_fletched_contrast_kernel(
         quant_h(1, BANKS - 1)
 
         size = {}
-        rest = {}
-        order = [(0, 0), (1, 0), (0, 1), (1, 1), (2, 0), (2, 1), (3, 0), (3, 1)]
+        started = []
 
-        def scores(m, h):
-            first = 2 * order.index((m, h)) % BANKS
+        def product(dst, words, dtype, scales, h, j0, width):
+            step = HALF if width == HALF else JB
+            pieces = [(b, c) for b in range(HP) for c in range(0, width, step)]
+            for b, c in pieces:
+                cols = slice(j0 + c, j0 + c + step)
+                nc.tensor.matmul_mx(
+                    out=dst[:, c : c + step], lhsT=words[b].bitcast(dtype), lhsT_scale=scales[b],
+                    rhs=hq_w[b, h][:, cols].bitcast(FP8X4), rhs_scale=hq_s[b, h][:, cols],
+                    start=((b, c) == pieces[0]), stop=((b, c) == pieces[-1]))
+
+        def scores(m, first, width):
+            h, j0 = divmod(first, HALF)
+            bank = 2 * len(started) % BANKS
+            started.append((m, first))
+            rows = slice(m * P, (m + 1) * P)
             abs_e = ring.tile([P, HALF], F32, name="abs_e", bufs=4)
             abs_f = ring.tile([P, HALF], F32, name="abs_f", bufs=4)
-            f_ps = psum.tile([P, HALF], F32, name="bank%d" % first)
-            e_ps = psum.tile([P, HALF], F32, name="bank%d" % (first + 1))
-            for b in range(HP):
-                nc.tensor.matmul_mx(
-                    out=f_ps[:], lhsT=w4_w[:, b, 2 * m * P : 2 * (m + 1) * P].bitcast(FP4X4),
-                    lhsT_scale=w4_s[:, b, m * P : (m + 1) * P],
-                    rhs=hq_w[b, h][:].bitcast(FP8X4), rhs_scale=hq_s[b, h][:],
-                    start=(b == 0), stop=(b == HP - 1))
-            for b in range(HP):
-                nc.tensor.matmul_mx(
-                    out=e_ps[:], lhsT=v2_w[b][:, m * P : (m + 1) * P].bitcast(FP8X4),
-                    lhsT_scale=v2_s[4 * b :, m * P : (m + 1) * P],
-                    rhs=hq_w[b, h][:].bitcast(FP8X4), rhs_scale=hq_s[b, h][:],
-                    start=(b == 0), stop=(b == HP - 1))
-            nc.scalar.activation(out=abs_f[:], in_=f_ps[:], func=ACT.Abs)
-            nc.scalar.activation(out=abs_e[:], in_=e_ps[:], func=ACT.Abs)
-            if h == 0:
+            f_ps = psum.tile([P, HALF], F32, name="bank%d" % bank)
+            e_ps = psum.tile([P, HALF], F32, name="bank%d" % (bank + 1))
+            product(f_ps, [w4_w[:, b, 2 * m * P : 2 * (m + 1) * P] for b in range(HP)], FP4X4,
+                    [w4_s[:, b, rows] for b in range(HP)], h, j0, width)
+            product(e_ps, [v2_w[b][:, rows] for b in range(HP)], FP8X4,
+                    [v2_s[4 * b :, rows] for b in range(HP)], h, j0, width)
+            nc.scalar.activation(out=abs_f[:, :width], in_=f_ps[:, :width], func=ACT.Abs)
+            nc.scalar.activation(out=abs_e[:, :width], in_=e_ps[:, :width], func=ACT.Abs)
+            if first == 0:
                 size[m] = ring.tile([P, S], F32, name="size", bufs=3)
-            nc.vector.tensor_tensor(out=size[m][:, h * HALF : (h + 1) * HALF], in0=abs_e[:], in1=abs_f[:], op=ALU.mult)
+            engine = nc.vector if len(started) <= 4 else nc.gpsimd
+            engine.tensor_tensor(out=size[m][:, first : first + width], in0=abs_e[:, :width],
+                                 in1=abs_f[:, :width], op=ALU.mult)
 
-        fletched = {}
-
-        def pick_fletched(m):
-            fletched[m] = ring.tile([P, NP], F32, name="fletched")
-            nc.vector.tensor_copy(fletched[m][:], size[m][:].indirect(pos2_sb[:]))
-
-        def offset_fletched(m):
-            rest[m] = ring.tile([P, NP], F32, name="rest")
-            nc.scalar.activation(out=rest[m][:], in_=fletched[m][:], func=ACT.Identity,
-                                 bias=set_sb[:, m : m + 1], scale=-1.0)
-
-        def pick_bare(m):
+        def contrast(m):
+            fletched = ring.tile([P, NP], F32, name="fletched")
+            bare = ring.tile([P, NP], F32, name="bare")
             res = ring.tile([P, NP], F32, name="res")
-            nc.vector.tensor_tensor(out=res[:], in0=size[m][:].indirect(pos1_sb[:]), in1=rest[m][:], op=ALU.add)
+            nc.vector.tensor_copy(fletched[:], size[m][:].indirect(pos2_sb[:]))
+            nc.vector.tensor_copy(bare[:], size[m][:].indirect(pos1_sb[:]))
+            nc.vector.scalar_tensor_tensor(out=res[:], in0=bare[:], scalar=set_sb[:, m : m + 1], in1=fletched[:],
+                                           op0=ALU.add, op1=ALU.subtract)
             nc.sync.dma_start(out=out[m * P : (m + 1) * P, :], in_=res[:])
 
-        scores(0, 0)
-        scores(1, 0)
-        scores(0, 1)
-        pick_fletched(0)
-        scores(1, 1)
-        offset_fletched(0)
-        pick_fletched(1)
-        pick_bare(0)
-        scores(2, 0)
-        scores(2, 1)
-        offset_fletched(1)
-        pick_fletched(2)
-        pick_bare(1)
-        scores(3, 0)
-        scores(3, 1)
-        offset_fletched(2)
-        pick_fletched(3)
-        offset_fletched(3)
-        pick_bare(2)
-        pick_bare(3)
+        scores(0, 0, HALF)
+        scores(1, 0, HALF)
+        scores(0, HALF, HALF - JB)
+        scores(0, S - JB, JB)
+        scores(1, HALF, HALF)
+        contrast(0)
+        scores(2, 0, HALF)
+        scores(2, HALF, HALF)
+        contrast(1)
+        scores(3, 0, HALF)
+        scores(3, HALF, HALF)
+        contrast(2)
+        contrast(3)

@@ -65,7 +65,7 @@ def tile_list_bare_fletched_contrast_kernel(
             nc.sync.dma_start(out=w_raw[b, a][:], in_=rows.rearrange("(p i) c -> p i c", i=PACK))
 
         for q in range(4):
-            nc.gpsimd.dma_start(out=tab_s[32 * q : 32 * q + 4 * KP, :].bitcast(I32),
+            nc.gpsimd.dma_start(out=tab_s[32 * q + 4 : 32 * q + 4 + 4 * KP, :].bitcast(I32),
                                 in_=tab_scales[:, 4 * q : 4 * q + 4, :].bitcast(I32))
         for q in range(4):
             nc.gpsimd.dma_start(out=tab2_s[32 * q : 32 * q + 4 * HP, :].bitcast(I32),
@@ -133,31 +133,30 @@ def tile_list_bare_fletched_contrast_kernel(
                     lhsT=wq_w[b, a][:, t * P : (t + 1) * P].bitcast(FP8X4),
                     lhsT_scale=wq_s[b, a][:, t * P : (t + 1) * P],
                     rhs=v_w[a][h][:, j0 : j0 + JB].bitcast(FP8X4),
-                    rhs_scale=v_s[4 * a :, jb * JB : (jb + 1) * JB],
+                    rhs_scale=v_s[4 * (a + 1) :, jb * JB : (jb + 1) * JB],
                     start=(a == 0 and t == 0),
                     stop=(a == KP - 1 and t == PACK - 1),
                 )
 
         h_bf = {}
 
-        def features(b, jb):
+        def features(b, jb, banks):
             h, j0 = divmod(jb * JB, HALF)
             if j0 == 0:
                 h_bf[b, h] = ring.tile([P, HALF, PACK], BF16, name="h_bf", align_bytes=64)
-            th = ring.tile([P, JB, PACK], F32, name="th", bufs=6)
-            nc.scalar.activation(out=th[:], in_=pre[b, jb][:].rearrange("p t j -> p j t"), func=ACT.Tanh)
-            nc.vector.tensor_tensor(out=h_bf[b, h][:, j0 : j0 + JB, :], in0=th[:],
-                                    in1=gain_sb[:, b : b + 1, :].to_broadcast([P, JB, PACK]), op=ALU.mult)
+            width = banks * JB
+            th = ring.tile([P, 2 * JB, PACK], F32, name="th", bufs=4)
+            for u in range(banks):
+                nc.scalar.activation(out=th[:, u * JB : (u + 1) * JB, :],
+                                     in_=pre[b, jb + u][:].rearrange("p t j -> p j t"), func=ACT.Tanh)
+            nc.vector.tensor_tensor(out=h_bf[b, h][:, j0 : j0 + width, :], in0=th[:, :width, :],
+                                    in1=gain_sb[:, b : b + 1, :].to_broadcast([P, width, PACK]), op=ALU.mult)
 
-        def quant_h(b, jb):
+        def quant_h(b, jb, banks):
             h, j0 = divmod(jb * JB, HALF)
-            nc.vector.quantize_mx(out=hq_w[b, h][:, j0 : j0 + JB].bitcast(FP8X4), scales=hq_s[b, h][:, j0 : j0 + JB],
-                                  in_=h_bf[b, h][:, j0 : j0 + JB, :].rearrange("p j t -> p (j t)"))
-
-        def feature_step(b, jb):
-            features(b, jb)
-            if jb > 0:
-                quant_h(b, jb - 1)
+            cols = slice(j0, j0 + banks * JB)
+            nc.vector.quantize_mx(out=hq_w[b, h][:, cols].bitcast(FP8X4), scales=hq_s[b, h][:, cols],
+                                  in_=h_bf[b, h][:, cols, :].rearrange("p j t -> p (j t)"))
 
         gather_v(0, 0)
         gather_v(0, 1)
@@ -176,27 +175,28 @@ def tile_list_bare_fletched_contrast_kernel(
             for jb in range(BANKS):
                 stage1(0, a, jb)
         cast_w1(1, 0, True)
-        feature_step(0, 0)
+        features(0, 0, 2)
         quant_w1(1, 0)
-        for jb in range(1, 4):
-            feature_step(0, jb)
+        features(0, 2, 2)
         cast_w1(1, 1, False)
-        feature_step(0, 4)
+        features(0, 4, 2)
         quant_w1(1, 1)
-        for jb in range(5, BANKS):
-            feature_step(0, jb)
+        quant_h(0, 0, 4)
+        features(0, 6, 2)
         cast_w1(1, 2, False)
         nc.vector.tensor_copy(v2_s[:], tab2_s[:].indirect(offs2_sb[:]))
-        quant_h(0, BANKS - 1)
         quant_w1(1, 2)
+        quant_h(0, 4, 4)
         nc.vector.tensor_copy(v2_w[0][:], tab2_w[0][:].indirect(offs2_sb[:]))
         nc.vector.tensor_copy(v2_w[1][:], tab2_w[1][:].indirect(offs2_sb[:]))
         for jb in range(BANKS):
             for a in range(KP):
                 stage1(1, a, jb)
         for jb in range(BANKS):
-            feature_step(1, jb)
-        quant_h(1, BANKS - 1)
+            features(1, jb, 1)
+            if jb > 0:
+                quant_h(1, jb - 1, 1)
+        quant_h(1, BANKS - 1, 1)
 
         size = {}
         started = []
@@ -228,9 +228,10 @@ def tile_list_bare_fletched_contrast_kernel(
             nc.scalar.activation(out=abs_e[:, :width], in_=e_ps[:, :width], func=ACT.Abs)
             if first == 0:
                 size[m] = ring.tile([P, S], F32, name="size", bufs=3)
-            engine = nc.vector if len(started) <= 4 else nc.gpsimd
+            engine = nc.gpsimd if 4 < len(started) < 9 else nc.vector
             engine.tensor_tensor(out=size[m][:, first : first + width], in0=abs_e[:, :width],
                                  in1=abs_f[:, :width], op=ALU.mult)
+            return abs_e, abs_f
 
         def contrast(m):
             fletched = ring.tile([P, NP], F32, name="fletched")
@@ -240,6 +241,18 @@ def tile_list_bare_fletched_contrast_kernel(
             nc.vector.tensor_copy(bare[:], size[m][:].indirect(pos1_sb[:]))
             nc.vector.scalar_tensor_tensor(out=res[:], in0=bare[:], scalar=set_sb[:, m : m + 1], in1=fletched[:],
                                            op0=ALU.add, op1=ALU.subtract)
+            nc.sync.dma_start(out=out[m * P : (m + 1) * P, :], in_=res[:])
+
+        def pick_fletched(m):
+            fletched = ring.tile([P, NP], F32, name="fletched")
+            nc.vector.tensor_copy(fletched[:], size[m][:].indirect(pos2_sb[:]))
+            return fletched
+
+        def add_bare(m, fletched, rest):
+            res = ring.tile([P, NP], F32, name="res")
+            nc.scalar.activation(out=rest[:], in_=fletched[:], func=ACT.Identity,
+                                 bias=set_sb[:, m : m + 1], scale=-1.0)
+            nc.vector.tensor_tensor(out=res[:], in0=size[m][:].indirect(pos1_sb[:]), in1=rest[:], op=ALU.add)
             nc.sync.dma_start(out=out[m * P : (m + 1) * P, :], in_=res[:])
 
         scores(0, 0, HALF)
@@ -252,6 +265,7 @@ def tile_list_bare_fletched_contrast_kernel(
         scores(2, HALF, HALF)
         contrast(1)
         scores(3, 0, HALF)
-        scores(3, HALF, HALF)
-        contrast(2)
-        contrast(3)
+        spent = scores(3, HALF, HALF)
+        picked = [pick_fletched(m) for m in (2, 3)]
+        add_bare(2, picked[0], spent[0])
+        add_bare(3, picked[1], spent[1])

from contextlib import ExitStack

import concourse.mybir as mybir

K, H, T, S, T3, S2, NP = 1536, 1024, 4096, 1024, 2048, 512, 512
FLOPS = 2 * K * H * S + 2 * 2 * H * S2 * S

F32 = mybir.dt.float32
BF16 = mybir.dt.bfloat16
I32 = mybir.dt.int32
U32 = mybir.dt.uint32
U16 = mybir.dt.uint16
U8 = mybir.dt.uint8
FP8X4 = mybir.dt.float8_e4m3fn_x4
FP4X4 = mybir.dt.float4_e2m1fn_x4
ACT = mybir.ActivationFunctionType
ALU = mybir.AluOpType

P = 128
PACK = 4
PASS = P * PACK
KP = K // PASS
HP = H // PASS
BANKS = 8
JB = S // BANKS
HALF = 512
MT = S2 // P


def tile_list_bare_fletched_contrast_kernel(
    tc, tab_words, tab_scales, offs, tab2_words, tab2_scales, offs2, pos1, pos2,
    w1, gain, w4_words, w4_scales, setting, out,
):
    nc = tc.nc
    with ExitStack() as ctx:
        keep = ctx.enter_context(tc.tile_pool(name="keep", bufs=1))
        ring = ctx.enter_context(tc.tile_pool(name="ring", bufs=2))
        psum = ctx.enter_context(tc.psum_pool(name="psum", bufs=1))

        def kept(shape, dtype, name):
            return keep.tile(shape, dtype, name=name, align_bytes=64)

        offs_sb = keep.tile([P, S // 16], U16, name="offs_sb")
        offs2_sb = keep.tile([P, S2 // 16], U16, name="offs2_sb")
        pos1_sb = keep.tile([P, NP // 16], U16, name="pos1_sb")
        pos2_sb = keep.tile([P, NP // 16], U16, name="pos2_sb")
        tab_w = [kept([P, T], U32, "tab_w%d" % a) for a in range(KP)]
        tab_s = kept([P, T], U8, "tab_s")
        tab2_w = [kept([P, T3], U32, "tab2_w%d" % b) for b in range(HP)]
        tab2_s = kept([P, T3], U8, "tab2_s")
        w4_w = kept([P, HP, 2 * S2], U8, "w4_w")
        w4_s = kept([P, HP, S2], U8, "w4_s")
        w_raw = {(b, a): kept([P, PACK, PASS], F32, "w_raw%d%d" % (b, a)) for b in range(HP) for a in range(KP)}
        gain_sb = kept([P, HP, PACK], F32, "gain_sb")
        set_sb = kept([P, MT], F32, "set_sb")

        nc.vector.memset(tab_s[:].bitcast(I32), 0)
        nc.vector.memset(tab2_s[:].bitcast(I32), 0)
        nc.vector.memset(w4_s[:].rearrange("p a n -> p (a n)").bitcast(I32), 0)
        def load_words(dst, src):
            nc.sync.dma_start(out=dst[:].bitcast(I32), in_=src.rearrange("p n t -> p (n t)").bitcast(I32))

        def load_w1(b, a):
            rows = w1[a * PASS : (a + 1) * PASS, b * PASS : (b + 1) * PASS]
            nc.sync.dma_start(out=w_raw[b, a][:], in_=rows.rearrange("(p i) c -> p i c", i=PACK))

        for q in range(4):
            nc.gpsimd.dma_start(out=tab_s[32 * q + 4 : 32 * q + 4 + 4 * KP, :].bitcast(I32),
                                in_=tab_scales[:, 4 * q : 4 * q + 4, :].bitcast(I32))
        for q in range(4):
            nc.gpsimd.dma_start(out=tab2_s[32 * q : 32 * q + 4 * HP, :].bitcast(I32),
                                in_=tab2_scales[:, 4 * q : 4 * q + 4, :].bitcast(I32))
        for q in range(4):
            nc.gpsimd.dma_start(out=w4_s[32 * q : 32 * q + 4, :, :].bitcast(I32),
                                in_=w4_scales[:, 4 * q : 4 * q + 4, :].rearrange("a r n -> r a n").bitcast(I32))
        load_words(tab_w[0], tab_words[0])
        nc.sync.dma_start(offs_sb[:], offs)
        load_w1(0, 0)
        nc.sync.dma_start(offs2_sb[:], offs2)
        load_w1(0, 1)
        nc.sync.dma_start(out=gain_sb[:], in_=gain.rearrange("(b p t) -> p b t", p=P, t=PACK))
        load_words(tab_w[1], tab_words[1])
        load_w1(0, 2)
        load_words(tab_w[2], tab_words[2])
        load_w1(1, 0)
        load_w1(1, 1)
        load_w1(1, 2)
        nc.sync.dma_start(out=w4_w[:].bitcast(I32), in_=w4_words.rearrange("a p n -> p a n").bitcast(I32))
        load_words(tab2_w[0], tab2_words[0])
        load_words(tab2_w[1], tab2_words[1])
        nc.sync.dma_start(pos2_sb[:], pos2)
        nc.sync.dma_start(pos1_sb[:], pos1)
        with nc.allow_non_contiguous_dma(reason="one offset a partition"):
            nc.sync.dma_start(out=set_sb[:], in_=setting.rearrange("(m p) -> p m", p=P))

        v_w = [[kept([P, HALF], U32, "v_w%d%d" % (a, h)) for h in range(2)] for a in range(KP)]
        v_s = kept([P, S], U8, "v_s")
        v2_w = [kept([P, S2], U32, "v2_w%d" % b) for b in range(HP)]
        v2_s = kept([P, S2], U8, "v2_s")
        wq_w = {key: kept([P, PASS], U32, "wq_w%d%d" % key) for key in w_raw}
        wq_s = {key: kept([P, PASS], U8, "wq_s%d%d" % key) for key in w_raw}
        hq_w = {(b, h): kept([P, HALF], U32, "hq_w%d%d" % (b, h)) for b in range(HP) for h in range(2)}
        hq_s = {(b, h): kept([P, HALF], U8, "hq_s%d%d" % (b, h)) for b in range(HP) for h in range(2)}

        def gather_v(a, h):
            cols = HALF // 16
            nc.vector.tensor_copy(v_w[a][h][:], tab_w[a][:].indirect(offs_sb[:, h * cols : (h + 1) * cols]))

        w_bf = {}

        def cast_w1(b, a, on_vector):
            w_bf[b, a] = ring.tile([P, PACK, P, PACK], BF16, name="w_bf", align_bytes=64)
            src = w_raw[b, a][:].rearrange("p i (m u v) -> p u m i v", u=2, v=2)
            dst = w_bf[b, a][:].rearrange("p (u v) m i -> p u m i v", v=2)
            if on_vector:
                nc.vector.tensor_copy(out=dst, in_=src)
            else:
                nc.scalar.copy(out=dst, in_=src)

        def quant_w1(b, a):
            nc.vector.quantize_mx(out=wq_w[b, a][:].bitcast(FP8X4), scales=wq_s[b, a][:],
                                  in_=w_bf[b, a][:].rearrange("p t m i -> p (t m i)"))

        pre = {}

        def stage1(b, a, jb):
            if a == 0:
                pre[b, jb] = psum.tile([P, PACK, JB], F32, name="bank%d" % jb)
            h, j0 = divmod(jb * JB, HALF)
            for t in range(PACK):
                nc.tensor.matmul_mx(
                    out=pre[b, jb][:, t, :],
                    lhsT=wq_w[b, a][:, t * P : (t + 1) * P].bitcast(FP8X4),
                    lhsT_scale=wq_s[b, a][:, t * P : (t + 1) * P],
                    rhs=v_w[a][h][:, j0 : j0 + JB].bitcast(FP8X4),
                    rhs_scale=v_s[4 * (a + 1) :, jb * JB : (jb + 1) * JB],
                    start=(a == 0 and t == 0),
                    stop=(a == KP - 1 and t == PACK - 1),
                )

        h_bf = {}

        def features(b, jb, banks):
            h, j0 = divmod(jb * JB, HALF)
            if j0 == 0:
                h_bf[b, h] = ring.tile([P, HALF, PACK], BF16, name="h_bf", align_bytes=64)
            width = banks * JB
            th = ring.tile([P, 2 * JB, PACK], F32, name="th", bufs=4)
            for u in range(banks):
                nc.scalar.activation(out=th[:, u * JB : (u + 1) * JB, :],
                                     in_=pre[b, jb + u][:].rearrange("p t j -> p j t"), func=ACT.Tanh)
            nc.vector.tensor_tensor(out=h_bf[b, h][:, j0 : j0 + width, :], in0=th[:, :width, :],
                                    in1=gain_sb[:, b : b + 1, :].to_broadcast([P, width, PACK]), op=ALU.mult)

        def quant_h(b, jb, banks):
            h, j0 = divmod(jb * JB, HALF)
            cols = slice(j0, j0 + banks * JB)
            nc.vector.quantize_mx(out=hq_w[b, h][:, cols].bitcast(FP8X4), scales=hq_s[b, h][:, cols],
                                  in_=h_bf[b, h][:, cols, :].rearrange("p j t -> p (j t)"))

        gather_v(0, 0)
        gather_v(0, 1)
        cast_w1(0, 0, False)
        quant_w1(0, 0)
        nc.vector.tensor_copy(v_s[:], tab_s[:].indirect(offs_sb[:]))
        cast_w1(0, 1, False)
        quant_w1(0, 1)
        gather_v(1, 0)
        gather_v(1, 1)
        cast_w1(0, 2, False)
        quant_w1(0, 2)
        gather_v(2, 0)
        gather_v(2, 1)
        for a in range(KP):
            for jb in range(BANKS):
                stage1(0, a, jb)
        cast_w1(1, 0, True)
        features(0, 0, 2)
        quant_w1(1, 0)
        features(0, 2, 2)
        cast_w1(1, 1, False)
        features(0, 4, 2)
        quant_w1(1, 1)
        quant_h(0, 0, 4)
        features(0, 6, 2)
        cast_w1(1, 2, False)
        nc.vector.tensor_copy(v2_s[:], tab2_s[:].indirect(offs2_sb[:]))
        quant_w1(1, 2)
        quant_h(0, 4, 4)
        nc.vector.tensor_copy(v2_w[0][:], tab2_w[0][:].indirect(offs2_sb[:]))
        nc.vector.tensor_copy(v2_w[1][:], tab2_w[1][:].indirect(offs2_sb[:]))
        for jb in range(BANKS):
            for a in range(KP):
                stage1(1, a, jb)
        for jb in range(BANKS):
            features(1, jb, 1)
            if jb > 0:
                quant_h(1, jb - 1, 1)
        quant_h(1, BANKS - 1, 1)

        size = {}
        started = []

        def product(dst, words, dtype, scales, h, j0, width):
            step = HALF if width == HALF else JB
            pieces = [(b, c) for b in range(HP) for c in range(0, width, step)]
            for b, c in pieces:
                cols = slice(j0 + c, j0 + c + step)
                nc.tensor.matmul_mx(
                    out=dst[:, c : c + step], lhsT=words[b].bitcast(dtype), lhsT_scale=scales[b],
                    rhs=hq_w[b, h][:, cols].bitcast(FP8X4), rhs_scale=hq_s[b, h][:, cols],
                    start=((b, c) == pieces[0]), stop=((b, c) == pieces[-1]))

        def scores(m, first, width):
            h, j0 = divmod(first, HALF)
            bank = 2 * len(started) % BANKS
            started.append((m, first))
            rows = slice(m * P, (m + 1) * P)
            abs_e = ring.tile([P, HALF], F32, name="abs_e", bufs=4)
            abs_f = ring.tile([P, HALF], F32, name="abs_f", bufs=4)
            f_ps = psum.tile([P, HALF], F32, name="bank%d" % bank)
            e_ps = psum.tile([P, HALF], F32, name="bank%d" % (bank + 1))
            product(f_ps, [w4_w[:, b, 2 * m * P : 2 * (m + 1) * P] for b in range(HP)], FP4X4,
                    [w4_s[:, b, rows] for b in range(HP)], h, j0, width)
            product(e_ps, [v2_w[b][:, rows] for b in range(HP)], FP8X4,
                    [v2_s[4 * b :, rows] for b in range(HP)], h, j0, width)
            nc.scalar.activation(out=abs_f[:, :width], in_=f_ps[:, :width], func=ACT.Abs)
            nc.scalar.activation(out=abs_e[:, :width], in_=e_ps[:, :width], func=ACT.Abs)
            if first == 0:
                size[m] = ring.tile([P, S], F32, name="size", bufs=3)
            engine = nc.gpsimd if 4 < len(started) < 9 else nc.vector
            engine.tensor_tensor(out=size[m][:, first : first + width], in0=abs_e[:, :width],
                                 in1=abs_f[:, :width], op=ALU.mult)
            return abs_e, abs_f

        def contrast(m):
            fletched = ring.tile([P, NP], F32, name="fletched")
            bare = ring.tile([P, NP], F32, name="bare")
            res = ring.tile([P, NP], F32, name="res")
            nc.vector.tensor_copy(fletched[:], size[m][:].indirect(pos2_sb[:]))
            nc.vector.tensor_copy(bare[:], size[m][:].indirect(pos1_sb[:]))
            nc.vector.scalar_tensor_tensor(out=res[:], in0=bare[:], scalar=set_sb[:, m : m + 1], in1=fletched[:],
                                           op0=ALU.add, op1=ALU.subtract)
            nc.sync.dma_start(out=out[m * P : (m + 1) * P, :], in_=res[:])

        def pick_fletched(m):
            fletched = ring.tile([P, NP], F32, name="fletched")
            nc.vector.tensor_copy(fletched[:], size[m][:].indirect(pos2_sb[:]))
            return fletched

        def add_bare(m, fletched, rest):
            res = ring.tile([P, NP], F32, name="res")
            nc.scalar.activation(out=rest[:], in_=fletched[:], func=ACT.Identity,
                                 bias=set_sb[:, m : m + 1], scale=-1.0)
            nc.vector.tensor_tensor(out=res[:], in0=size[m][:].indirect(pos1_sb[:]), in1=rest[:], op=ALU.add)
            nc.sync.dma_start(out=out[m * P : (m + 1) * P, :], in_=res[:])

        scores(0, 0, HALF)
        scores(1, 0, HALF)
        scores(0, HALF, HALF - JB)
        scores(0, S - JB, JB)
        scores(1, HALF, HALF)
        contrast(0)
        scores(2, 0, HALF)
        scores(2, HALF, HALF)
        contrast(1)
        scores(3, 0, HALF)
        spent = scores(3, HALF, HALF)
        picked = [pick_fletched(m) for m in (2, 3)]
        add_bare(2, picked[0], spent[0])
        add_bare(3, picked[1], spent[1])
